import numpy as np
import ml_dtypes


def mxq(x, axis, fmt="e4m3"):
    dtype, down = {"e4m3": (ml_dtypes.float8_e4m3fn, 7), "e5m2": (ml_dtypes.float8_e5m2, 14)}[fmt]
    v = np.moveaxis(np.asarray(x, np.float32).astype(ml_dtypes.bfloat16).astype(np.float64), axis, -1)
    blocks = v.reshape(v.shape[:-1] + (-1, 32))
    amax = np.abs(blocks).max(-1, keepdims=True)
    byte = np.maximum(np.where(amax > 0, np.frexp(amax)[1] - 1 + 127, 0) - down, 1)
    scale = np.exp2(byte - 127.0)
    codes = (blocks / scale).astype(np.float32).astype(dtype).astype(np.float64)
    return np.moveaxis((codes * scale).reshape(v.shape), -1, axis)


WIDE = False


def mx_kscale(k):
    if not WIDE:
        return np.ones(k)
    levels = np.array([10, -10, 5, -5, 0])
    if k % 512:
        return np.exp2(np.random.permutation(np.resize(levels, k // 32))).repeat(32)
    a = np.empty((k // 512, 16))
    for p in range(k // 512):
        a[p, :8] = np.random.permutation(np.resize(levels, 8))
        for g in range(8):
            far = levels[np.abs(levels - a[p, g]) >= 10]
            a[p, g + 8] = far[np.random.randint(len(far))]
    return np.exp2(a.ravel()).repeat(32)


def f64(x):
    return np.asarray(x).astype(np.float64)


def striped(idx):
    return np.tile(idx.reshape(-1, 16).T, (8, 1)).astype(np.uint16)


def unstriped(offs):
    return offs[:16].T.reshape(-1).astype(np.int64)


E2M1 = np.array([0.0, 0.5, 1.0, 1.5, 2.0, 3.0, 4.0, 6.0, -0.0, -0.5, -1.0, -1.5, -2.0, -3.0, -4.0, -6.0])


def pack_weight(w, fmt):
    k, n = w.shape
    w = f64(np.asarray(w, np.float32).astype(ml_dtypes.bfloat16)).reshape(k // 32, 32, n)
    amax = np.abs(w).max(1)
    if fmt == "e4m3":
        byte = np.frexp(amax)[1] - 1 + 127 - 7
    else:
        mant, ex = np.frexp(amax / 6.0)
        byte = np.where(mant > 0.5, ex, ex - 1) + 127
    byte = np.clip(np.where(amax > 0, byte, 1), 1, 254)
    scaled = (w * np.exp2(127.0 - byte)[:, None, :]).reshape(k, n).astype(np.float32)
    by_word = np.ascontiguousarray(scaled.reshape(k // 512, 128, 4, n).transpose(0, 1, 3, 2))
    if fmt == "e4m3":
        words = by_word.astype(ml_dtypes.float8_e4m3fn).view(np.uint8)
    else:
        c = by_word.astype(ml_dtypes.float4_e2m1fn).view(np.uint8) & 0xF
        words = (c[..., 0::2] | (c[..., 1::2] << 4)).reshape(k // 512, 128, 2 * n)
    return np.ascontiguousarray(words), np.ascontiguousarray(byte.astype(np.uint8).reshape(k // 512, 16, n))


def unpack_weight(words, scales, fmt):
    g, _, n = scales.shape
    words = np.ascontiguousarray(words).reshape(g, 128, n, -1)
    if fmt == "e4m3":
        vals = words.view(ml_dtypes.float8_e4m3fn).astype(np.float64)
    else:
        nib = np.empty((g, 128, n, 4), np.uint8)
        nib[..., 0::2] = words & 0xF
        nib[..., 1::2] = words >> 4
        vals = E2M1[nib]
    vals = vals * np.repeat(np.exp2(scales.astype(np.float64) - 127.0), 8, axis=1)[..., None]
    return vals.transpose(0, 1, 3, 2).reshape(g * 512, n)


def gelu(v):
    return 0.5 * v * (1.0 + np.tanh(np.sqrt(2.0 / np.pi) * (v + 0.044715 * v**3)))


K, T, S, H, T2, P = 1024, 4096, 1024, 1024, 2048, 512

def setup_inputs():
    n = np.random.standard_normal
    s = mx_kscale(K)[:, None]
    u = mx_kscale(H)[:, None]
    d = {}
    d["tab_words"], d["tab_scales"] = pack_weight(n((K, T)) * s, "e4m3")
    d["offs"] = striped(np.random.permutation(T)[:S])
    d["w1"] = (n((K, H)) / s * u.T / K**0.5).astype(np.float32)
    d["b1"] = (0.8 * n(H) * u[:, 0]).astype(np.float32)
    d["wgs"] = np.exp(0.3 * n((128, S))).astype(np.float32)
    d["page0"] = (n((H, T2)) * u).astype(np.float32)
    d["offs2"] = striped(np.random.permutation(T2)[:S])
    d["offs3"] = striped(np.random.permutation(T2)[:P])
    d["offs4"] = striped(np.random.permutation(T2)[:P])
    d["cue"] = (1.3 * np.exp(0.2 * n(H)) / u[:, 0]).astype(np.float32)
    d["gain"] = (np.exp(0.3 * n(H)) * u[:, 0]).astype(np.float32)
    d["w4_words"], d["w4_scales"] = pack_weight(1.5 * n((H, H)) / u / H**0.5, "e2m1")
    d["near"] = (0.7 * np.exp(0.3 * n(H)) / u[:, 0]).astype(np.float32)
    return d

def reference(tab_words, tab_scales, offs, w1, b1, wgs, page0, offs2, offs3, offs4, cue, gain, w4_words, w4_scales, near):
    v = unpack_weight(tab_words, tab_scales, "e4m3")[:, unstriped(offs)]
    h = (mxq(f64(w1), 0, "e4m3").T @ v) + f64(b1)[:, None]
    page = f64(page0).copy()
    page[:, unstriped(offs2)] = np.tile(f64(wgs), (H // 128, 1)) * h
    x = f64(gain)[:, None] * np.tanh(f64(cue)[:, None] * page[:, unstriped(offs3)])
    w4 = unpack_weight(w4_words, w4_scales, "e2m1")
    y = w4.T @ mxq(x, 0, "e4m3")
    out = y + f64(near)[:, None] * page[:, unstriped(offs4)]
    return out

@@ -1,0 +1,286 @@
+from contextlib import ExitStack
+
+import concourse.mybir as mybir
+from concourse.masks import make_identity
+
+K, T, S, H, T2, M = 1024, 4096, 1024, 1024, 2048, 512
+FLOPS = 2 * K * H * S + 2 * H * H * M
+
+F32 = mybir.dt.float32
+BF16 = mybir.dt.bfloat16
+I32 = mybir.dt.int32
+U32 = mybir.dt.uint32
+U16 = mybir.dt.uint16
+U8 = mybir.dt.uint8
+FP8X4 = mybir.dt.float8_e4m3fn_x4
+FP4X4 = mybir.dt.float4_e2m1fn_x4
+ACT = mybir.ActivationFunctionType
+ALU = mybir.AluOpType
+
+P = 128
+PACK = 4
+K_PASS = P * PACK
+PASSES = 2
+TILES = H // P
+BANK = 512
+W1_GROUPS = ((0, 1), (1, 3), (3, 8))
+
+
+def tile_list_firework_burst_board_kernel(
+    tc, tab_words, tab_scales, offs, w1, b1, wgs, page0, offs2, offs3, offs4,
+    cue, gain, w4_words, w4_scales, near, out,
+):
+    nc = tc.nc
+    with ExitStack() as ctx:
+        lists = ctx.enter_context(tc.tile_pool(name="lists", bufs=1))
+        keep = ctx.enter_context(tc.tile_pool(name="keep", bufs=1))
+        ring = ctx.enter_context(tc.tile_pool(name="ring", bufs=3))
+        psum = ctx.enter_context(tc.psum_pool(name="psum", bufs=1))
+
+        def bank(i, shape, dtype, name):
+            return psum.tile(shape, dtype, tag="bank%d" % i, name=name)
+
+        idx = lists.tile([P, S // 16], U16, name="idx")
+        idx2 = lists.tile([P, S // 16], U16, name="idx2")
+        idx3 = lists.tile([P, M // 16], U16, name="idx3")
+        idx4 = lists.tile([P, M // 16], U16, name="idx4")
+
+        tab = [keep.tile([P, T], I32, tag="tab%d" % a, name="tab%d" % a, align_bytes=64) for a in range(PASSES)]
+        tab_sc = keep.tile([P, T], U8, name="tab_sc")
+        w1_raw = [
+            keep.tile([P, PASSES, PACK, (hi - lo) * P], F32, tag="w1_raw%d" % g, name="w1_raw%d" % g)
+            for g, (lo, hi) in enumerate(W1_GROUPS)
+        ]
+        wgs_sb = keep.tile([P, S], F32, tag="wgs", name="wgs_sb")
+        page = [keep.tile([P, T2], F32, name="page%d" % c) for c in range(TILES)]
+        w4 = keep.tile([P, PASSES, 2 * H], U8, name="w4", align_bytes=64)
+        w4_sc = keep.tile([P, PASSES, H], U8, name="w4_sc", align_bytes=64)
+        vec_rows = keep.tile([P, P], F32, name="vec_rows")
+        vec_cols = keep.tile([P, 4 * TILES], F32, name="vec_cols")
+        ident_f32 = keep.tile([P, P], F32, name="ident_f32")
+        ident_bf16 = keep.tile([P, P], BF16, name="ident_bf16")
+
+        def load_tab(a):
+            nc.sync.dma_start(out=tab[a][:], in_=tab_words[a].rearrange("p t i -> p (t i)").bitcast(I32))
+
+        def load_w1(g):
+            lo, hi = W1_GROUPS[g]
+            for a in range(PASSES):
+                rows = w1[a * K_PASS : (a + 1) * K_PASS, lo * P : hi * P]
+                nc.sync.dma_start(out=w1_raw[g][:, a], in_=rows.rearrange("(p j) c -> p j c", j=PACK))
+
+        def load_page(c):
+            nc.sync.dma_start(out=page[c][:], in_=page0[c * P : (c + 1) * P, :])
+
+        nc.gpsimd.memset(vec_rows[:], 0.0)
+        nc.gpsimd.memset(tab_sc[:].bitcast(I32), 0)
+        for q in range(4):
+            nc.gpsimd.dma_start(
+                out=tab_sc[32 * q : 32 * q + 8, :].bitcast(I32),
+                in_=tab_scales[:, 4 * q : 4 * q + 4, :].bitcast(I32),
+            )
+        for v, vec in enumerate((b1, cue, gain, near)):
+            nc.scalar.dma_start(
+                out=vec_rows[v * TILES : (v + 1) * TILES, :], in_=vec.rearrange("(c p) -> c p", p=P)
+            )
+        make_identity(nc, ident_f32[:])
+        nc.gpsimd.memset(w4_sc[:].rearrange("p a n -> p (a n)").bitcast(I32), 0)
+        make_identity(nc, ident_bf16[:])
+
+        nc.sync.dma_start(out=idx[:], in_=offs)
+        load_tab(0)
+        load_w1(0)
+        load_tab(1)
+        nc.sync.dma_start(out=idx2[:], in_=offs2)
+        nc.sync.dma_start(out=wgs_sb[:, :BANK], in_=wgs[:, :BANK])
+        load_page(0)
+        nc.sync.dma_start(out=wgs_sb[:, BANK:], in_=wgs[:, BANK:])
+        nc.sync.dma_start(out=idx3[:], in_=offs3)
+        nc.sync.dma_start(out=idx4[:], in_=offs4)
+        load_w1(1)
+        load_page(1)
+        load_w1(2)
+        load_page(2)
+        nc.sync.dma_start(out=w4[:].bitcast(I32), in_=w4_words.rearrange("a p n -> p a n").bitcast(I32))
+        for q in range(4):
+            nc.sync.dma_start(
+                out=w4_sc[32 * q : 32 * q + 4].bitcast(I32),
+                in_=w4_scales[:, 4 * q : 4 * q + 4, :].rearrange("a r n -> r a n").bitcast(I32),
+            )
+        for c in range(3, TILES):
+            load_page(c)
+
+        vec_ps = bank(2, [P, P], F32, "vec_ps")
+        nc.tensor.transpose(vec_ps[:], vec_rows[:], ident_f32[:])
+        nc.scalar.activation(vec_cols[:], vec_ps[:, : 4 * TILES], ACT.Identity)
+
+        def col(v, c):
+            return vec_cols[:, v * TILES + c : v * TILES + c + 1]
+
+        v_words = [keep.tile([P, S], U32, name="v_words%d" % a, align_bytes=64) for a in range(PASSES)]
+        v_sc = keep.tile([P, S], U8, name="v_sc", align_bytes=64)
+        nc.vector.tensor_copy(v_words[0][:], tab[0][:].bitcast(U32).indirect(idx[:]))
+        nc.vector.tensor_copy(v_sc[:], tab_sc[:].indirect(idx[:]))
+
+        first_codes = keep.tile([P, PASSES * P], U32, tag="second", name="first_codes", align_bytes=64)
+        w1_codes = {0: first_codes[:]}
+        w1_sc = keep.tile([P, TILES, PASSES * P], U8, name="w1_sc", align_bytes=64)
+        w1_bf = {}
+
+        def cast_w1(c):
+            g = [i for i, (lo, hi) in enumerate(W1_GROUPS) if lo <= c < hi][0]
+            c0 = (c - W1_GROUPS[g][0]) * P
+            nc.scalar.copy(
+                w1_bf[c].rearrange("p (a n i t) -> p a n t i", a=PASSES, i=4, t=PACK),
+                w1_raw[g][:, :, :, c0 : c0 + P].rearrange("p a t (n i) -> p a n t i", i=4),
+            )
+
+        def quantize_w1(c):
+            nc.vector.quantize_mx(out=w1_codes[c].bitcast(FP8X4), scales=w1_sc[:, c, :], in_=w1_bf[c])
+
+        first_bf = keep.tile([P, K], BF16, name="first_bf", align_bytes=64)
+        w1_bf[0] = first_bf[:]
+        cast_w1(0)
+        quantize_w1(0)
+        for half in range(2):
+            nc.vector.tensor_copy(
+                v_words[1][:, half * BANK : (half + 1) * BANK],
+                tab[1][:].bitcast(U32).indirect(idx[:, half * 32 : (half + 1) * 32]),
+            )
+
+        h = {}
+
+        def make_h(c):
+            if c == 0:
+                h[c] = keep.tile([P, S], F32, tag="first_h", name="h0", align_bytes=64)
+            else:
+                h[c] = ring.tile([P, S], F32, tag="h", name="h%d" % c)
+            for half in range(2):
+                cols = slice(half * BANK, (half + 1) * BANK)
+                acc = bank(half, [P, BANK], F32, "h_ps%d_%d" % (c, half))
+                for a in range(PASSES):
+                    nc.tensor.matmul_mx(
+                        out=acc[:],
+                        lhsT=w1_codes[c][:, a * P : (a + 1) * P].bitcast(FP8X4),
+                        lhsT_scale=w1_sc[:, c, a * P : (a + 1) * P],
+                        rhs=v_words[a][:, cols].bitcast(FP8X4),
+                        rhs_scale=v_sc[4 * a :, cols],
+                        start=(a == 0),
+                        stop=(a == PASSES - 1),
+                    )
+                nc.scalar.activation(h[c][:, cols], acc[:], ACT.Identity, bias=col(0, c))
+
+        def scatter(c):
+            pieces = 2 if c < 2 else 1
+            n = S // pieces
+            for i in range(pieces):
+                nc.vector.tensor_tensor(
+                    page[c][:].indirect(idx2[:, i * n // 16 : (i + 1) * n // 16]),
+                    h[c][:, i * n : (i + 1) * n],
+                    wgs_sb[:, i * n : (i + 1) * n],
+                    ALU.mult,
+                )
+
+        make_h(0)
+        scatter(0)
+
+        second_bf = keep.tile([P, 2, K], BF16, tag="second", name="second_bf", align_bytes=64)
+        later_bf = keep.tile([P, TILES - 3, K], BF16, tag="tab1", name="later_bf", align_bytes=64)
+        second_codes = keep.tile([P, 2, PASSES * P], U32, tag="first_h", name="second_codes", align_bytes=64)
+        later_codes = keep.tile([P, TILES - 3, PASSES * P], U32, name="later_codes", align_bytes=64)
+        for c in range(1, 3):
+            w1_bf[c] = second_bf[:, c - 1, :]
+            w1_codes[c] = second_codes[:, c - 1, :]
+        for c in range(3, TILES):
+            w1_bf[c] = later_bf[:, c - 3, :]
+            w1_codes[c] = later_codes[:, c - 3, :]
+        for c in range(1, TILES):
+            cast_w1(c)
+            quantize_w1(c)
+
+        first_picks = keep.tile([P, 2, M], F32, tag="second", name="first_picks", align_bytes=64)
+        cued = keep.tile([P, TILES - 1, M], F32, tag="tab0", name="cued", align_bytes=64)
+        g3 = [first_picks[:, 0, :]] + [cued[:, c, :] for c in range(TILES - 1)]
+        g4 = {0: first_picks[:, 1, :]}
+
+        def pick4(c):
+            nc.vector.tensor_copy(g4[c], page[c][:].indirect(idx4[:]))
+
+        bounded = keep.tile([P, M], F32, tag="w1_raw2", name="bounded")
+        x_codes = keep.tile([P, PASSES, M], U32, name="x_codes", align_bytes=64)
+        x_sc = [keep.tile([P, M], U8, name="x_sc%d" % b, align_bytes=64) for b in range(PASSES)]
+        x_t = [keep.tile([P, 4, 2, P], F32, name="x_t%d" % b) for b in range(PASSES)]
+        x_q = [keep.tile([P, PACK * M], BF16, tag="x_q%d" % b, name="x_q%d" % b, align_bytes=64) for b in range(PASSES)]
+        y = {}
+        Y_BANK = (5, 6, 7, 0, 1, 2, 3, 4)
+
+        def y_pass(c, b):
+            if b == 0:
+                y[c] = bank(Y_BANK[c], [P, M], F32, "y%d" % c)
+            nc.tensor.matmul_mx(
+                out=y[c][:],
+                lhsT=w4[:, b, 2 * c * P : 2 * (c + 1) * P].bitcast(FP4X4),
+                lhsT_scale=w4_sc[:, b, c * P : (c + 1) * P],
+                rhs=x_codes[:, b, :].bitcast(FP8X4),
+                rhs_scale=x_sc[b][:],
+                start=(b == 0),
+                stop=(b == PASSES - 1),
+            )
+
+        def make_x(c):
+            b, cc = divmod(c, 4)
+            nc.scalar.activation(bounded[:], g3[c], ACT.Tanh, scale=col(1, c))
+            x_bf = ring.tile([P, M], BF16, tag="x_bf", name="x_bf%d" % c)
+            nc.scalar.activation(x_bf[:], bounded[:], ACT.Copy, scale=col(2, c))
+            turned = bank(2, [P, M], BF16, "turned%d" % c)
+            for k in range(4):
+                nc.tensor.transpose(turned[:, k * P : (k + 1) * P], x_bf[:, k * P : (k + 1) * P], ident_bf16[:])
+            nc.scalar.copy(
+                x_t[b][:, :, :, 32 * cc : 32 * (cc + 1)],
+                turned[:].bitcast(F32).rearrange("p (k q u) -> p k u q", k=4, u=2),
+            )
+
+        def quantize_x(b):
+            for j in range(2):
+                back = bank(3 + j, [P, 2, 2, P], F32, "back%d_%d" % (b, j))
+                for k in range(2):
+                    for u in range(2):
+                        nc.tensor.transpose(back[:, k, u, :], x_t[b][:, 2 * j + k, u, :], ident_f32[:])
+                nc.scalar.copy(
+                    x_q[b][:].bitcast(F32)[:, j * BANK : (j + 1) * BANK].rearrange("p (k m u) -> p k m u", k=2, u=2),
+                    back[:].rearrange("p k u m -> p k m u"),
+                )
+            nc.vector.quantize_mx(out=x_codes[:, b, :].bitcast(FP8X4), scales=x_sc[b][:], in_=x_q[b][:])
+
+        for c in range(TILES):
+            if c > 0:
+                scatter(c)
+            nc.vector.tensor_copy(g3[c], page[c][:].indirect(idx3[:]))
+            if c == 0:
+                pick4(0)
+            if c + 1 < TILES:
+                make_h(c + 1)
+            make_x(c)
+            if c == 3:
+                quantize_x(0)
+                for n in range(3):
+                    y_pass(n, 0)
+            if c == 6:
+                for n in range(3, 5):
+                    y_pass(n, 0)
+
+        mid_picks = keep.tile([P, 5, M], F32, tag="wgs", name="mid_picks")
+        for c in range(1, 6):
+            g4[c] = mid_picks[:, c - 1, :]
+            pick4(c)
+        quantize_x(1)
+        last_picks = keep.tile([P, 2, M], F32, tag="x_q1", name="last_picks", align_bytes=64)
+        for c in range(6, TILES):
+            g4[c] = last_picks[:, c - 6, :]
+            pick4(c)
+        for c in range(TILES):
+            if c >= 5:
+                y_pass(c, 0)
+            y_pass(c, 1)
+            nc.vector.scalar_tensor_tensor(g4[c], g4[c], col(3, c), y[c][:], ALU.mult, ALU.add)
+            nc.sync.dma_start(out=out[c * P : (c + 1) * P, :], in_=g4[c])

@@ -46,7 +46,7 @@ def tile_list_firework_burst_board_kernel(
         idx4 = lists.tile([P, M // 16], U16, name="idx4")
 
         tab = [keep.tile([P, T], I32, tag="tab%d" % a, name="tab%d" % a, align_bytes=64) for a in range(PASSES)]
-        tab_sc = keep.tile([P, T], U8, name="tab_sc")
+        tab_sc = keep.tile([P, T], U8, tag="tab_sc", name="tab_sc", align_bytes=64)
         w1_raw = [
             keep.tile([P, PASSES, PACK, (hi - lo) * P], F32, tag="w1_raw%d" % g, name="w1_raw%d" % g)
             for g, (lo, hi) in enumerate(W1_GROUPS)
@@ -72,8 +72,9 @@ def tile_list_firework_burst_board_kernel(
         def load_page(c):
             nc.sync.dma_start(out=page[c][:], in_=page0[c * P : (c + 1) * P, :])
 
-        nc.gpsimd.memset(vec_rows[:], 0.0)
-        nc.gpsimd.memset(tab_sc[:].bitcast(I32), 0)
+        nc.vector.memset(vec_rows[:], 0.0)
+        nc.vector.memset(tab_sc[:].bitcast(I32), 0)
+        nc.vector.memset(w4_sc[:].rearrange("p a n -> p (a n)").bitcast(I32), 0)
         for q in range(4):
             nc.gpsimd.dma_start(
                 out=tab_sc[32 * q : 32 * q + 8, :].bitcast(I32),
@@ -84,7 +85,6 @@ def tile_list_firework_burst_board_kernel(
                 out=vec_rows[v * TILES : (v + 1) * TILES, :], in_=vec.rearrange("(c p) -> c p", p=P)
             )
         make_identity(nc, ident_f32[:])
-        nc.gpsimd.memset(w4_sc[:].rearrange("p a n -> p (a n)").bitcast(I32), 0)
         make_identity(nc, ident_bf16[:])
 
         nc.sync.dma_start(out=idx[:], in_=offs)
@@ -95,9 +95,9 @@ def tile_list_firework_burst_board_kernel(
         nc.sync.dma_start(out=wgs_sb[:, :BANK], in_=wgs[:, :BANK])
         load_page(0)
         nc.sync.dma_start(out=wgs_sb[:, BANK:], in_=wgs[:, BANK:])
+        load_w1(1)
         nc.sync.dma_start(out=idx3[:], in_=offs3)
         nc.sync.dma_start(out=idx4[:], in_=offs4)
-        load_w1(1)
         load_page(1)
         load_w1(2)
         load_page(2)
@@ -117,7 +117,7 @@ def tile_list_firework_burst_board_kernel(
         def col(v, c):
             return vec_cols[:, v * TILES + c : v * TILES + c + 1]
 
-        v_words = [keep.tile([P, S], U32, name="v_words%d" % a, align_bytes=64) for a in range(PASSES)]
+        v_words = [keep.tile([P, S], U32, name="v_words0", align_bytes=64)]
         v_sc = keep.tile([P, S], U8, name="v_sc", align_bytes=64)
         nc.vector.tensor_copy(v_words[0][:], tab[0][:].bitcast(U32).indirect(idx[:]))
         nc.vector.tensor_copy(v_sc[:], tab_sc[:].indirect(idx[:]))
@@ -142,6 +142,7 @@ def tile_list_firework_burst_board_kernel(
         w1_bf[0] = first_bf[:]
         cast_w1(0)
         quantize_w1(0)
+        v_words.append(keep.tile([P, S], U32, tag="tab_sc", name="v_words1", align_bytes=64))
         for half in range(2):
             nc.vector.tensor_copy(
                 v_words[1][:, half * BANK : (half + 1) * BANK],
@@ -269,14 +270,14 @@ def tile_list_firework_burst_board_kernel(
                 for n in range(3, 5):
                     y_pass(n, 0)
 
-        mid_picks = keep.tile([P, 5, M], F32, tag="wgs", name="mid_picks")
-        for c in range(1, 6):
+        mid_picks = keep.tile([P, 6, M], F32, tag="wgs", name="mid_picks")
+        for c in range(1, 7):
             g4[c] = mid_picks[:, c - 1, :]
             pick4(c)
         quantize_x(1)
-        last_picks = keep.tile([P, 2, M], F32, tag="x_q1", name="last_picks", align_bytes=64)
-        for c in range(6, TILES):
-            g4[c] = last_picks[:, c - 6, :]
+        last_picks = keep.tile([P, 1, M], F32, tag="x_q1", name="last_picks", align_bytes=64)
+        for c in range(7, TILES):
+            g4[c] = last_picks[:, c - 7, :]
             pick4(c)
         for c in range(TILES):
             if c >= 5:

@@ -188,26 +188,30 @@ def tile_list_firework_burst_board_kernel(
         second_bf = keep.tile([P, 2, K], BF16, tag="second", name="second_bf", align_bytes=64)
         later_bf = keep.tile([P, TILES - 3, K], BF16, tag="tab1", name="later_bf", align_bytes=64)
         second_codes = keep.tile([P, 2, PASSES * P], U32, tag="first_h", name="second_codes", align_bytes=64)
-        later_codes = keep.tile([P, TILES - 3, PASSES * P], U32, name="later_codes", align_bytes=64)
         for c in range(1, 3):
             w1_bf[c] = second_bf[:, c - 1, :]
             w1_codes[c] = second_codes[:, c - 1, :]
         for c in range(3, TILES):
             w1_bf[c] = later_bf[:, c - 3, :]
-            w1_codes[c] = later_codes[:, c - 3, :]
+            w1_codes[c] = keep.tile(
+                [P, PASSES * P], U32, tag="codes%d" % c, name="codes%d" % c, align_bytes=64
+            )[:]
         for c in range(1, TILES):
             cast_w1(c)
             quantize_w1(c)
 
-        first_picks = keep.tile([P, 2, M], F32, tag="second", name="first_picks", align_bytes=64)
-        cued = keep.tile([P, TILES - 1, M], F32, tag="tab0", name="cued", align_bytes=64)
-        g3 = [first_picks[:, 0, :]] + [cued[:, c, :] for c in range(TILES - 1)]
+        first_picks = keep.tile([P, 2, M], F32, tag="w1_raw1", name="first_picks")
+        after_casts = keep.tile([P, 2, M], F32, tag="w1_raw2", name="after_casts")
+        g3 = {0: first_picks[:, 0, :], 1: after_casts[:, 0, :]}
         g4 = {0: first_picks[:, 1, :]}
+
+        def pick3(c):
+            nc.vector.tensor_copy(g3[c], page[c][:].indirect(idx3[:]))
 
         def pick4(c):
             nc.vector.tensor_copy(g4[c], page[c][:].indirect(idx4[:]))
 
-        bounded = keep.tile([P, M], F32, tag="w1_raw2", name="bounded")
+        bounded = after_casts[:, 1, :]
         x_codes = keep.tile([P, PASSES, M], U32, name="x_codes", align_bytes=64)
         x_sc = [keep.tile([P, M], U8, name="x_sc%d" % b, align_bytes=64) for b in range(PASSES)]
         x_t = [keep.tile([P, 4, 2, P], F32, name="x_t%d" % b) for b in range(PASSES)]
@@ -230,9 +234,9 @@ def tile_list_firework_burst_board_kernel(
 
         def make_x(c):
             b, cc = divmod(c, 4)
-            nc.scalar.activation(bounded[:], g3[c], ACT.Tanh, scale=col(1, c))
+            nc.scalar.activation(bounded, g3[c], ACT.Tanh, scale=col(1, c))
             x_bf = ring.tile([P, M], BF16, tag="x_bf", name="x_bf%d" % c)
-            nc.scalar.activation(x_bf[:], bounded[:], ACT.Copy, scale=col(2, c))
+            nc.scalar.activation(x_bf[:], bounded, ACT.Copy, scale=col(2, c))
             turned = bank(2, [P, M], BF16, "turned%d" % c)
             for k in range(4):
                 nc.tensor.transpose(turned[:, k * P : (k + 1) * P], x_bf[:, k * P : (k + 1) * P], ident_bf16[:])
@@ -253,22 +257,32 @@ def tile_list_firework_burst_board_kernel(
                 )
             nc.vector.quantize_mx(out=x_codes[:, b, :].bitcast(FP8X4), scales=x_sc[b][:], in_=x_q[b][:])
 
-        for c in range(TILES):
-            if c > 0:
-                scatter(c)
-            nc.vector.tensor_copy(g3[c], page[c][:].indirect(idx3[:]))
-            if c == 0:
-                pick4(0)
-            if c + 1 < TILES:
-                make_h(c + 1)
-            make_x(c)
-            if c == 3:
+        pick3(0)
+        pick4(0)
+        make_h(1)
+        for c in range(1, TILES - 1):
+            scatter(c)
+            make_h(c + 1)
+            if 3 <= c < TILES - 2:
+                g3[c - 1] = keep.tile([P, M], F32, tag="codes%d" % (c + 1), name="cued%d" % (c - 1), align_bytes=64)[:]
+            if c == TILES - 2:
+                last_two = keep.tile([P, 2, M], F32, tag="codes%d" % (c + 1), name="last_two", align_bytes=64)
+                g3[c - 1], g3[c] = last_two[:, 0, :], last_two[:, 1, :]
+            if c >= 2:
+                pick3(c - 1)
+            make_x(c - 1)
+            if c == 4:
                 quantize_x(0)
                 for n in range(3):
                     y_pass(n, 0)
-            if c == 6:
-                for n in range(3, 5):
-                    y_pass(n, 0)
+        pick3(6)
+        make_x(6)
+        for n in range(3, 5):
+            y_pass(n, 0)
+        scatter(7)
+        g3[7] = keep.tile([P, M], F32, name="cued7")[:]
+        pick3(7)
+        make_x(7)
 
         mid_picks = keep.tile([P, 6, M], F32, tag="wgs", name="mid_picks")
         for c in range(1, 7):

@@ -76,7 +76,8 @@ def tile_list_firework_burst_board_kernel(
         nc.vector.memset(tab_sc[:].bitcast(I32), 0)
         nc.vector.memset(w4_sc[:].rearrange("p a n -> p (a n)").bitcast(I32), 0)
         for q in range(4):
-            nc.gpsimd.dma_start(
+            queue = nc.scalar if q == 3 else nc.gpsimd
+            queue.dma_start(
                 out=tab_sc[32 * q : 32 * q + 8, :].bitcast(I32),
                 in_=tab_scales[:, 4 * q : 4 * q + 4, :].bitcast(I32),
             )
@@ -232,29 +233,36 @@ def tile_list_firework_burst_board_kernel(
                 stop=(b == PASSES - 1),
             )
 
-        def make_x(c):
+        def turn_out(c, x_bf, k0, nk, bank_no):
             b, cc = divmod(c, 4)
-            nc.scalar.activation(bounded, g3[c], ACT.Tanh, scale=col(1, c))
-            x_bf = ring.tile([P, M], BF16, tag="x_bf", name="x_bf%d" % c)
-            nc.scalar.activation(x_bf[:], bounded, ACT.Copy, scale=col(2, c))
-            turned = bank(2, [P, M], BF16, "turned%d" % c)
-            for k in range(4):
-                nc.tensor.transpose(turned[:, k * P : (k + 1) * P], x_bf[:, k * P : (k + 1) * P], ident_bf16[:])
+            cols = slice(k0 * P, (k0 + nk) * P)
+            nc.scalar.activation(bounded[:, cols], g3[c][:, cols], ACT.Tanh, scale=col(1, c))
+            nc.scalar.activation(x_bf[:, cols], bounded[:, cols], ACT.Copy, scale=col(2, c))
+            turned = bank(bank_no, [P, nk * P], BF16, "turned%d_%d" % (c, k0))
+            for k in range(nk):
+                nc.tensor.transpose(
+                    turned[:, k * P : (k + 1) * P], x_bf[:, (k0 + k) * P : (k0 + k + 1) * P], ident_bf16[:]
+                )
             nc.scalar.copy(
-                x_t[b][:, :, :, 32 * cc : 32 * (cc + 1)],
-                turned[:].bitcast(F32).rearrange("p (k q u) -> p k u q", k=4, u=2),
+                x_t[b][:, k0 : k0 + nk, :, 32 * cc : 32 * (cc + 1)],
+                turned[:].bitcast(F32).rearrange("p (k q u) -> p k u q", k=nk, u=2),
+            )
+
+        def make_x(c):
+            x_bf = ring.tile([P, M], BF16, tag="x_bf", name="x_bf%d" % c)
+            turn_out(c, x_bf, 0, 4, 2)
+
+        def turn_back(b, j):
+            back = bank(3 + j, [P, 2, 2, P], F32, "back%d_%d" % (b, j))
+            for k in range(2):
+                for u in range(2):
+                    nc.tensor.transpose(back[:, k, u, :], x_t[b][:, 2 * j + k, u, :], ident_f32[:])
+            nc.scalar.copy(
+                x_q[b][:].bitcast(F32)[:, j * BANK : (j + 1) * BANK].rearrange("p (k m u) -> p k m u", k=2, u=2),
+                back[:].rearrange("p k u m -> p k m u"),
             )
 
         def quantize_x(b):
-            for j in range(2):
-                back = bank(3 + j, [P, 2, 2, P], F32, "back%d_%d" % (b, j))
-                for k in range(2):
-                    for u in range(2):
-                        nc.tensor.transpose(back[:, k, u, :], x_t[b][:, 2 * j + k, u, :], ident_f32[:])
-                nc.scalar.copy(
-                    x_q[b][:].bitcast(F32)[:, j * BANK : (j + 1) * BANK].rearrange("p (k m u) -> p k m u", k=2, u=2),
-                    back[:].rearrange("p k u m -> p k m u"),
-                )
             nc.vector.quantize_mx(out=x_codes[:, b, :].bitcast(FP8X4), scales=x_sc[b][:], in_=x_q[b][:])
 
         pick3(0)
@@ -272,17 +280,25 @@ def tile_list_firework_burst_board_kernel(
                 pick3(c - 1)
             make_x(c - 1)
             if c == 4:
+                for j in range(2):
+                    turn_back(0, j)
                 quantize_x(0)
                 for n in range(3):
                     y_pass(n, 0)
         pick3(6)
         make_x(6)
-        for n in range(3, 5):
+        for n in range(3, 6):
             y_pass(n, 0)
         scatter(7)
         g3[7] = keep.tile([P, M], F32, name="cued7")[:]
-        pick3(7)
-        make_x(7)
+        x_bf7 = ring.tile([P, M], BF16, tag="x_bf", name="x_bf7")
+        for j in range(2):
+            nc.vector.tensor_copy(
+                g3[7][:, j * M // 2 : (j + 1) * M // 2], page[7][:].indirect(idx3[:, j * 16 : (j + 1) * 16])
+            )
+        for j in range(2):
+            turn_out(7, x_bf7, 2 * j, 2, 3 + j)
+            turn_back(1, j)
 
         mid_picks = keep.tile([P, 6, M], F32, tag="wgs", name="mid_picks")
         for c in range(1, 7):
@@ -294,7 +310,7 @@ def tile_list_firework_burst_board_kernel(
             g4[c] = last_picks[:, c - 7, :]
             pick4(c)
         for c in range(TILES):
-            if c >= 5:
+            if c >= 6:
                 y_pass(c, 0)
             y_pass(c, 1)
             nc.vector.scalar_tensor_tensor(g4[c], g4[c], col(3, c), y[c][:], ALU.mult, ALU.add)

@@ -212,10 +212,13 @@ def tile_list_firework_burst_board_kernel(
         def pick4(c):
             nc.vector.tensor_copy(g4[c], page[c][:].indirect(idx4[:]))
 
+        def scale4(c):
+            nc.scalar.activation(scaled[c], g4[c], ACT.Copy, scale=col(3, c))
+
         bounded = after_casts[:, 1, :]
         x_codes = keep.tile([P, PASSES, M], U32, name="x_codes", align_bytes=64)
         x_sc = [keep.tile([P, M], U8, name="x_sc%d" % b, align_bytes=64) for b in range(PASSES)]
-        x_t = [keep.tile([P, 4, 2, P], F32, name="x_t%d" % b) for b in range(PASSES)]
+        x_t = [keep.tile([P, 4, 2, P], F32, tag="x_t%d" % b, name="x_t%d" % b) for b in range(PASSES)]
         x_q = [keep.tile([P, PACK * M], BF16, tag="x_q%d" % b, name="x_q%d" % b, align_bytes=64) for b in range(PASSES)]
         y = {}
         Y_BANK = (5, 6, 7, 0, 1, 2, 3, 4)
@@ -268,6 +271,7 @@ def tile_list_firework_burst_board_kernel(
         pick3(0)
         pick4(0)
         make_h(1)
+        scaled = {}
         for c in range(1, TILES - 1):
             scatter(c)
             make_h(c + 1)
@@ -279,6 +283,9 @@ def tile_list_firework_burst_board_kernel(
             if c >= 2:
                 pick3(c - 1)
             make_x(c - 1)
+            if c == 2:
+                scaled[0] = g4[0]
+                scale4(0)
             if c == 4:
                 for j in range(2):
                     turn_back(0, j)
@@ -300,18 +307,42 @@ def tile_list_firework_burst_board_kernel(
             turn_out(7, x_bf7, 2 * j, 2, 3 + j)
             turn_back(1, j)
 
-        mid_picks = keep.tile([P, 6, M], F32, tag="wgs", name="mid_picks")
-        for c in range(1, 7):
+        mid_picks = keep.tile([P, 5, M], F32, tag="wgs", name="mid_picks")
+        for c in range(1, 6):
             g4[c] = mid_picks[:, c - 1, :]
             pick4(c)
         quantize_x(1)
-        last_picks = keep.tile([P, 1, M], F32, tag="x_q1", name="last_picks", align_bytes=64)
-        for c in range(7, TILES):
-            g4[c] = last_picks[:, c - 7, :]
-            pick4(c)
-        for c in range(TILES):
-            if c >= 6:
-                y_pass(c, 0)
+        g4[6] = keep.tile([P, M], F32, tag="x_q1", name="last_pick", align_bytes=64)[:]
+        mid_scaled = keep.tile([P, 5, M], F32, tag="x_t1", name="mid_scaled")
+        y_sb = keep.tile([P, 2, M], F32, name="y_sb")
+        for c in range(1, 6):
+            scaled[c] = mid_scaled[:, c - 1, :]
+        scaled[6] = g4[6]
+        pick4(6)
+        for c in range(6, TILES):
+            y_pass(c, 0)
+        for c in (0, 2, 1, 3, 4, 5, 6, 7):
             y_pass(c, 1)
-            nc.vector.scalar_tensor_tensor(g4[c], g4[c], col(3, c), y[c][:], ALU.mult, ALU.add)
-            nc.sync.dma_start(out=out[c * P : (c + 1) * P, :], in_=g4[c])
+
+        def finish(c):
+            if c in (2, 3):
+                nc.gpsimd.tensor_tensor(scaled[c], scaled[c], y_sb[:, c - 2, :], ALU.add)
+            else:
+                nc.vector.tensor_tensor(scaled[c], scaled[c], y[c][:], ALU.add)
+            queue = nc.scalar if c == 3 else nc.sync
+            queue.dma_start(out=out[c * P : (c + 1) * P, :], in_=scaled[c])
+
+        scale4(1)
+        scale4(2)
+        for c in (2, 3):
+            nc.scalar.copy(y_sb[:, c - 2, :], y[c][:])
+        scale4(3)
+        finish(0)
+        finish(1)
+        g4[7] = g4[3]
+        scaled[7] = g4[7]
+        pick4(7)
+        for c in range(4, TILES):
+            scale4(c)
+        for c in (2, 4, 5, 6, 7, 3):
+            finish(c)

from contextlib import ExitStack

import concourse.mybir as mybir
from concourse.masks import make_identity

K, T, S, H, T2, M = 1024, 4096, 1024, 1024, 2048, 512
FLOPS = 2 * K * H * S + 2 * H * H * M

F32 = mybir.dt.float32
BF16 = mybir.dt.bfloat16
I32 = mybir.dt.int32
U32 = mybir.dt.uint32
U16 = mybir.dt.uint16
U8 = mybir.dt.uint8
FP8X4 = mybir.dt.float8_e4m3fn_x4
FP4X4 = mybir.dt.float4_e2m1fn_x4
ACT = mybir.ActivationFunctionType
ALU = mybir.AluOpType

P = 128
PACK = 4
K_PASS = P * PACK
PASSES = 2
TILES = H // P
BANK = 512
W1_GROUPS = ((0, 1), (1, 3), (3, 8))


def tile_list_firework_burst_board_kernel(
    tc, tab_words, tab_scales, offs, w1, b1, wgs, page0, offs2, offs3, offs4,
    cue, gain, w4_words, w4_scales, near, out,
):
    nc = tc.nc
    with ExitStack() as ctx:
        lists = ctx.enter_context(tc.tile_pool(name="lists", bufs=1))
        keep = ctx.enter_context(tc.tile_pool(name="keep", bufs=1))
        ring = ctx.enter_context(tc.tile_pool(name="ring", bufs=3))
        psum = ctx.enter_context(tc.psum_pool(name="psum", bufs=1))

        def bank(i, shape, dtype, name):
            return psum.tile(shape, dtype, tag="bank%d" % i, name=name)

        idx = lists.tile([P, S // 16], U16, name="idx")
        idx2 = lists.tile([P, S // 16], U16, name="idx2")
        idx3 = lists.tile([P, M // 16], U16, name="idx3")
        idx4 = lists.tile([P, M // 16], U16, name="idx4")

        tab = [keep.tile([P, T], I32, tag="tab%d" % a, name="tab%d" % a, align_bytes=64) for a in range(PASSES)]
        tab_sc = keep.tile([P, T], U8, tag="tab_sc", name="tab_sc", align_bytes=64)
        w1_raw = [
            keep.tile([P, PASSES, PACK, (hi - lo) * P], F32, tag="w1_raw%d" % g, name="w1_raw%d" % g)
            for g, (lo, hi) in enumerate(W1_GROUPS)
        ]
        wgs_sb = keep.tile([P, S], F32, tag="wgs", name="wgs_sb")
        page = [keep.tile([P, T2], F32, name="page%d" % c) for c in range(TILES)]
        w4 = keep.tile([P, PASSES, 2 * H], U8, name="w4", align_bytes=64)
        w4_sc = keep.tile([P, PASSES, H], U8, name="w4_sc", align_bytes=64)
        vec_rows = keep.tile([P, P], F32, name="vec_rows")
        vec_cols = keep.tile([P, 4 * TILES], F32, name="vec_cols")
        ident_f32 = keep.tile([P, P], F32, name="ident_f32")
        ident_bf16 = keep.tile([P, P], BF16, name="ident_bf16")

        def load_tab(a):
            nc.sync.dma_start(out=tab[a][:], in_=tab_words[a].rearrange("p t i -> p (t i)").bitcast(I32))

        def load_w1(g):
            lo, hi = W1_GROUPS[g]
            for a in range(PASSES):
                rows = w1[a * K_PASS : (a + 1) * K_PASS, lo * P : hi * P]
                nc.sync.dma_start(out=w1_raw[g][:, a], in_=rows.rearrange("(p j) c -> p j c", j=PACK))

        def load_page(c):
            nc.sync.dma_start(out=page[c][:], in_=page0[c * P : (c + 1) * P, :])

        nc.vector.memset(vec_rows[:], 0.0)
        nc.vector.memset(tab_sc[:].bitcast(I32), 0)
        nc.vector.memset(w4_sc[:].rearrange("p a n -> p (a n)").bitcast(I32), 0)
        for q in range(4):
            queue = nc.scalar if q == 3 else nc.gpsimd
            queue.dma_start(
                out=tab_sc[32 * q : 32 * q + 8, :].bitcast(I32),
                in_=tab_scales[:, 4 * q : 4 * q + 4, :].bitcast(I32),
            )
        for v, vec in enumerate((b1, cue, gain, near)):
            nc.scalar.dma_start(
                out=vec_rows[v * TILES : (v + 1) * TILES, :], in_=vec.rearrange("(c p) -> c p", p=P)
            )
        make_identity(nc, ident_f32[:])
        make_identity(nc, ident_bf16[:])

        nc.sync.dma_start(out=idx[:], in_=offs)
        load_tab(0)
        load_w1(0)
        load_tab(1)
        nc.sync.dma_start(out=idx2[:], in_=offs2)
        nc.sync.dma_start(out=wgs_sb[:, :BANK], in_=wgs[:, :BANK])
        load_page(0)
        nc.sync.dma_start(out=wgs_sb[:, BANK:], in_=wgs[:, BANK:])
        load_w1(1)
        nc.sync.dma_start(out=idx3[:], in_=offs3)
        nc.sync.dma_start(out=idx4[:], in_=offs4)
        load_page(1)
        load_w1(2)
        load_page(2)
        nc.sync.dma_start(out=w4[:].bitcast(I32), in_=w4_words.rearrange("a p n -> p a n").bitcast(I32))
        for q in range(4):
            nc.sync.dma_start(
                out=w4_sc[32 * q : 32 * q + 4].bitcast(I32),
                in_=w4_scales[:, 4 * q : 4 * q + 4, :].rearrange("a r n -> r a n").bitcast(I32),
            )
        for c in range(3, TILES):
            load_page(c)

        vec_ps = bank(2, [P, P], F32, "vec_ps")
        nc.tensor.transpose(vec_ps[:], vec_rows[:], ident_f32[:])
        nc.scalar.activation(vec_cols[:], vec_ps[:, : 4 * TILES], ACT.Identity)

        def col(v, c):
            return vec_cols[:, v * TILES + c : v * TILES + c + 1]

        v_words = [keep.tile([P, S], U32, name="v_words0", align_bytes=64)]
        v_sc = keep.tile([P, S], U8, name="v_sc", align_bytes=64)
        nc.vector.tensor_copy(v_words[0][:], tab[0][:].bitcast(U32).indirect(idx[:]))
        nc.vector.tensor_copy(v_sc[:], tab_sc[:].indirect(idx[:]))

        first_codes = keep.tile([P, PASSES * P], U32, tag="second", name="first_codes", align_bytes=64)
        w1_codes = {0: first_codes[:]}
        w1_sc = keep.tile([P, TILES, PASSES * P], U8, name="w1_sc", align_bytes=64)
        w1_bf = {}

        def cast_w1(c):
            g = [i for i, (lo, hi) in enumerate(W1_GROUPS) if lo <= c < hi][0]
            c0 = (c - W1_GROUPS[g][0]) * P
            nc.scalar.copy(
                w1_bf[c].rearrange("p (a n i t) -> p a n t i", a=PASSES, i=4, t=PACK),
                w1_raw[g][:, :, :, c0 : c0 + P].rearrange("p a t (n i) -> p a n t i", i=4),
            )

        def quantize_w1(c):
            nc.vector.quantize_mx(out=w1_codes[c].bitcast(FP8X4), scales=w1_sc[:, c, :], in_=w1_bf[c])

        first_bf = keep.tile([P, K], BF16, name="first_bf", align_bytes=64)
        w1_bf[0] = first_bf[:]
        cast_w1(0)
        quantize_w1(0)
        v_words.append(keep.tile([P, S], U32, tag="tab_sc", name="v_words1", align_bytes=64))
        for half in range(2):
            nc.vector.tensor_copy(
                v_words[1][:, half * BANK : (half + 1) * BANK],
                tab[1][:].bitcast(U32).indirect(idx[:, half * 32 : (half + 1) * 32]),
            )

        h = {}

        def make_h(c):
            if c == 0:
                h[c] = keep.tile([P, S], F32, tag="first_h", name="h0", align_bytes=64)
            else:
                h[c] = ring.tile([P, S], F32, tag="h", name="h%d" % c)
            for half in range(2):
                cols = slice(half * BANK, (half + 1) * BANK)
                acc = bank(half, [P, BANK], F32, "h_ps%d_%d" % (c, half))
                for a in range(PASSES):
                    nc.tensor.matmul_mx(
                        out=acc[:],
                        lhsT=w1_codes[c][:, a * P : (a + 1) * P].bitcast(FP8X4),
                        lhsT_scale=w1_sc[:, c, a * P : (a + 1) * P],
                        rhs=v_words[a][:, cols].bitcast(FP8X4),
                        rhs_scale=v_sc[4 * a :, cols],
                        start=(a == 0),
                        stop=(a == PASSES - 1),
                    )
                nc.scalar.activation(h[c][:, cols], acc[:], ACT.Identity, bias=col(0, c))

        def scatter(c):
            pieces = 2 if c < 2 else 1
            n = S // pieces
            for i in range(pieces):
                nc.vector.tensor_tensor(
                    page[c][:].indirect(idx2[:, i * n // 16 : (i + 1) * n // 16]),
                    h[c][:, i * n : (i + 1) * n],
                    wgs_sb[:, i * n : (i + 1) * n],
                    ALU.mult,
                )

        make_h(0)
        scatter(0)

        second_bf = keep.tile([P, 2, K], BF16, tag="second", name="second_bf", align_bytes=64)
        later_bf = keep.tile([P, TILES - 3, K], BF16, tag="tab1", name="later_bf", align_bytes=64)
        second_codes = keep.tile([P, 2, PASSES * P], U32, tag="first_h", name="second_codes", align_bytes=64)
        for c in range(1, 3):
            w1_bf[c] = second_bf[:, c - 1, :]
            w1_codes[c] = second_codes[:, c - 1, :]
        for c in range(3, TILES):
            w1_bf[c] = later_bf[:, c - 3, :]
            w1_codes[c] = keep.tile(
                [P, PASSES * P], U32, tag="codes%d" % c, name="codes%d" % c, align_bytes=64
            )[:]
        for c in range(1, TILES):
            cast_w1(c)
            quantize_w1(c)

        first_picks = keep.tile([P, 2, M], F32, tag="w1_raw1", name="first_picks")
        after_casts = keep.tile([P, 2, M], F32, tag="w1_raw2", name="after_casts")
        g3 = {0: first_picks[:, 0, :], 1: after_casts[:, 0, :]}
        g4 = {0: first_picks[:, 1, :]}

        def pick3(c):
            nc.vector.tensor_copy(g3[c], page[c][:].indirect(idx3[:]))

        def pick4(c):
            nc.vector.tensor_copy(g4[c], page[c][:].indirect(idx4[:]))

        def scale4(c):
            nc.scalar.activation(scaled[c], g4[c], ACT.Copy, scale=col(3, c))

        bounded = after_casts[:, 1, :]
        x_codes = keep.tile([P, PASSES, M], U32, name="x_codes", align_bytes=64)
        x_sc = [keep.tile([P, M], U8, name="x_sc%d" % b, align_bytes=64) for b in range(PASSES)]
        x_t = [keep.tile([P, 4, 2, P], F32, tag="x_t%d" % b, name="x_t%d" % b) for b in range(PASSES)]
        x_q = [keep.tile([P, PACK * M], BF16, tag="x_q%d" % b, name="x_q%d" % b, align_bytes=64) for b in range(PASSES)]
        y = {}
        Y_BANK = (5, 6, 7, 0, 1, 2, 3, 4)

        def y_pass(c, b):
            if b == 0:
                y[c] = bank(Y_BANK[c], [P, M], F32, "y%d" % c)
            nc.tensor.matmul_mx(
                out=y[c][:],
                lhsT=w4[:, b, 2 * c * P : 2 * (c + 1) * P].bitcast(FP4X4),
                lhsT_scale=w4_sc[:, b, c * P : (c + 1) * P],
                rhs=x_codes[:, b, :].bitcast(FP8X4),
                rhs_scale=x_sc[b][:],
                start=(b == 0),
                stop=(b == PASSES - 1),
            )

        def turn_out(c, x_bf, k0, nk, bank_no):
            b, cc = divmod(c, 4)
            cols = slice(k0 * P, (k0 + nk) * P)
            nc.scalar.activation(bounded[:, cols], g3[c][:, cols], ACT.Tanh, scale=col(1, c))
            nc.scalar.activation(x_bf[:, cols], bounded[:, cols], ACT.Copy, scale=col(2, c))
            turned = bank(bank_no, [P, nk * P], BF16, "turned%d_%d" % (c, k0))
            for k in range(nk):
                nc.tensor.transpose(
                    turned[:, k * P : (k + 1) * P], x_bf[:, (k0 + k) * P : (k0 + k + 1) * P], ident_bf16[:]
                )
            nc.scalar.copy(
                x_t[b][:, k0 : k0 + nk, :, 32 * cc : 32 * (cc + 1)],
                turned[:].bitcast(F32).rearrange("p (k q u) -> p k u q", k=nk, u=2),
            )

        def make_x(c):
            x_bf = ring.tile([P, M], BF16, tag="x_bf", name="x_bf%d" % c)
            turn_out(c, x_bf, 0, 4, 2)

        def turn_back(b, j):
            back = bank(3 + j, [P, 2, 2, P], F32, "back%d_%d" % (b, j))
            for k in range(2):
                for u in range(2):
                    nc.tensor.transpose(back[:, k, u, :], x_t[b][:, 2 * j + k, u, :], ident_f32[:])
            nc.scalar.copy(
                x_q[b][:].bitcast(F32)[:, j * BANK : (j + 1) * BANK].rearrange("p (k m u) -> p k m u", k=2, u=2),
                back[:].rearrange("p k u m -> p k m u"),
            )

        def quantize_x(b):
            nc.vector.quantize_mx(out=x_codes[:, b, :].bitcast(FP8X4), scales=x_sc[b][:], in_=x_q[b][:])

        pick3(0)
        pick4(0)
        make_h(1)
        scaled = {}
        for c in range(1, TILES - 1):
            scatter(c)
            make_h(c + 1)
            if 3 <= c < TILES - 2:
                g3[c - 1] = keep.tile([P, M], F32, tag="codes%d" % (c + 1), name="cued%d" % (c - 1), align_bytes=64)[:]
            if c == TILES - 2:
                last_two = keep.tile([P, 2, M], F32, tag="codes%d" % (c + 1), name="last_two", align_bytes=64)
                g3[c - 1], g3[c] = last_two[:, 0, :], last_two[:, 1, :]
            if c >= 2:
                pick3(c - 1)
            make_x(c - 1)
            if c == 2:
                scaled[0] = g4[0]
                scale4(0)
            if c == 4:
                for j in range(2):
                    turn_back(0, j)
                quantize_x(0)
                for n in range(3):
                    y_pass(n, 0)
        pick3(6)
        make_x(6)
        for n in range(3, 6):
            y_pass(n, 0)
        scatter(7)
        g3[7] = keep.tile([P, M], F32, name="cued7")[:]
        x_bf7 = ring.tile([P, M], BF16, tag="x_bf", name="x_bf7")
        for j in range(2):
            nc.vector.tensor_copy(
                g3[7][:, j * M // 2 : (j + 1) * M // 2], page[7][:].indirect(idx3[:, j * 16 : (j + 1) * 16])
            )
        for j in range(2):
            turn_out(7, x_bf7, 2 * j, 2, 3 + j)
            turn_back(1, j)

        mid_picks = keep.tile([P, 5, M], F32, tag="wgs", name="mid_picks")
        for c in range(1, 6):
            g4[c] = mid_picks[:, c - 1, :]
            pick4(c)
        quantize_x(1)
        g4[6] = keep.tile([P, M], F32, tag="x_q1", name="last_pick", align_bytes=64)[:]
        mid_scaled = keep.tile([P, 5, M], F32, tag="x_t1", name="mid_scaled")
        y_sb = keep.tile([P, 2, M], F32, name="y_sb")
        for c in range(1, 6):
            scaled[c] = mid_scaled[:, c - 1, :]
        scaled[6] = g4[6]
        pick4(6)
        for c in range(6, TILES):
            y_pass(c, 0)
        for c in (0, 2, 1, 3, 4, 5, 6, 7):
            y_pass(c, 1)

        def finish(c):
            if c in (2, 3):
                nc.gpsimd.tensor_tensor(scaled[c], scaled[c], y_sb[:, c - 2, :], ALU.add)
            else:
                nc.vector.tensor_tensor(scaled[c], scaled[c], y[c][:], ALU.add)
            queue = nc.scalar if c == 3 else nc.sync
            queue.dma_start(out=out[c * P : (c + 1) * P, :], in_=scaled[c])

        scale4(1)
        scale4(2)
        for c in (2, 3):
            nc.scalar.copy(y_sb[:, c - 2, :], y[c][:])
        scale4(3)
        finish(0)
        finish(1)
        g4[7] = g4[3]
        scaled[7] = g4[7]
        pick4(7)
        for c in range(4, TILES):
            scale4(c)
        for c in (2, 4, 5, 6, 7, 3):
            finish(c)
